import numpy as np
import ml_dtypes


def mxq(x, axis, fmt="e4m3"):
    dtype, down = {"e4m3": (ml_dtypes.float8_e4m3fn, 7), "e5m2": (ml_dtypes.float8_e5m2, 14)}[fmt]
    v = np.moveaxis(np.asarray(x, np.float32).astype(ml_dtypes.bfloat16).astype(np.float64), axis, -1)
    blocks = v.reshape(v.shape[:-1] + (-1, 32))
    amax = np.abs(blocks).max(-1, keepdims=True)
    byte = np.maximum(np.where(amax > 0, np.frexp(amax)[1] - 1 + 127, 0) - down, 1)
    scale = np.exp2(byte - 127.0)
    codes = (blocks / scale).astype(np.float32).astype(dtype).astype(np.float64)
    return np.moveaxis((codes * scale).reshape(v.shape), -1, axis)


WIDE = False


def mx_kscale(k):
    if not WIDE:
        return np.ones(k)
    levels = np.array([10, -10, 5, -5, 0])
    if k % 512:
        return np.exp2(np.random.permutation(np.resize(levels, k // 32))).repeat(32)
    a = np.empty((k // 512, 16))
    for p in range(k // 512):
        a[p, :8] = np.random.permutation(np.resize(levels, 8))
        for g in range(8):
            far = levels[np.abs(levels - a[p, g]) >= 10]
            a[p, g + 8] = far[np.random.randint(len(far))]
    return np.exp2(a.ravel()).repeat(32)


def f64(x):
    return np.asarray(x).astype(np.float64)


def striped(idx):
    return np.tile(np.asarray(idx).reshape(-1, 16).T, (8, 1)).astype(np.uint16)


def unstriped(offs):
    return offs[:16].T.reshape(-1).astype(np.int64)


E2M1 = np.array([0.0, 0.5, 1.0, 1.5, 2.0, 3.0, 4.0, 6.0, -0.0, -0.5, -1.0, -1.5, -2.0, -3.0, -4.0, -6.0])


def pack_weight(w, fmt):
    k, n = w.shape
    w = f64(np.asarray(w, np.float32).astype(ml_dtypes.bfloat16)).reshape(k // 32, 32, n)
    amax = np.abs(w).max(1)
    if fmt == "e4m3":
        byte = np.frexp(amax)[1] - 1 + 127 - 7
    else:
        mant, ex = np.frexp(amax / 6.0)
        byte = np.where(mant > 0.5, ex, ex - 1) + 127
    byte = np.clip(np.where(amax > 0, byte, 1), 1, 254)
    scaled = (w * np.exp2(127.0 - byte)[:, None, :]).reshape(k, n).astype(np.float32)
    by_word = np.ascontiguousarray(scaled.reshape(k // 512, 128, 4, n).transpose(0, 1, 3, 2))
    if fmt == "e4m3":
        words = by_word.astype(ml_dtypes.float8_e4m3fn).view(np.uint8)
    else:
        c = by_word.astype(ml_dtypes.float4_e2m1fn).view(np.uint8) & 0xF
        words = (c[..., 0::2] | (c[..., 1::2] << 4)).reshape(k // 512, 128, 2 * n)
    return np.ascontiguousarray(words), np.ascontiguousarray(byte.astype(np.uint8).reshape(k // 512, 16, n))


def unpack_weight(words, scales, fmt):
    g, _, n = scales.shape
    words = np.ascontiguousarray(words).reshape(g, 128, n, -1)
    if fmt == "e4m3":
        vals = words.view(ml_dtypes.float8_e4m3fn).astype(np.float64)
    else:
        nib = np.empty((g, 128, n, 4), np.uint8)
        nib[..., 0::2] = words & 0xF
        nib[..., 1::2] = words >> 4
        vals = E2M1[nib]
    vals = vals * np.repeat(np.exp2(scales.astype(np.float64) - 127.0), 8, axis=1)[..., None]
    return vals.transpose(0, 1, 3, 2).reshape(g * 512, n)


D, T, I, Q, E, M = 512, 2048, 512, 256, 512, 1024


def setup_inputs():
    n = np.random.standard_normal
    idx = np.random.permutation(T)[:I]
    idx2 = np.random.permutation(T)[:I]
    idx3 = np.random.permutation(M)[:Q]
    fd = mx_kscale(D)
    fi = mx_kscale(I)
    ti = np.ones(T)
    ti[idx] = fi
    keysp = pack_weight(n((D, T)) / fd[:, None], "e4m3")
    return {
        "query": (n((D, Q)) * 1.0 / np.sqrt(D) * fd[:, None]).astype(np.float32),
        "keys_words": keysp[0],
        "keys_scales": keysp[1],
        "os": (np.random.uniform(0.02, 0.08, (1, I)) * fi).astype(np.float32),
        "vals": (n((E, T)) / ti).astype(np.float32),
        "member": (n((E, M))).astype(np.float32),
        "mgain": np.tile(np.random.uniform(0.5, 2.0, M), (128, 1)).astype(np.float32),
        "offs": striped(idx),
        "offs2": striped(idx2),
        "offs3": striped(idx3),
    }


def reference(query, keys_words, keys_scales, os, vals, member, mgain, offs, offs2, offs3):
    idx = unstriped(offs)
    idx2 = unstriped(offs2)
    idx3 = unstriped(offs3)
    keysu = unpack_weight(keys_words, keys_scales, "e4m3")
    queryq = mxq(f64(query), 0, "e4m3")
    a = queryq.T @ keysu
    s = a[:, idx] - a[:, idx2]
    w = np.maximum(s, 0.0)
    wo1 = w * f64(os)
    wt1 = wo1.T
    vt1 = f64(vals)[:, idx].T
    vt1q = mxq(vt1, 0, "e4m3")
    wt1q = mxq(wt1, 0, "e4m3")
    o = vt1q.T @ wt1q
    y = o * f64(mgain)[:1][:, idx3] + f64(member)[:, idx3]
    return y

@@ -1,0 +1,253 @@
+from contextlib import ExitStack
+
+import concourse.mybir as mybir
+
+D, T, I, Q, E, M = 512, 2048, 512, 256, 512, 1024
+FLOPS = 2 * D * Q * T + 2 * I * E * Q
+
+F32 = mybir.dt.float32
+BF16 = mybir.dt.bfloat16
+I32 = mybir.dt.int32
+U32 = mybir.dt.uint32
+U16 = mybir.dt.uint16
+U8 = mybir.dt.uint8
+FP8X4 = mybir.dt.float8_e4m3fn_x4
+ALU = mybir.AluOpType
+COPY = mybir.ActivationFunctionType.Copy
+
+P = 128
+PACK = 4
+BANK = 512
+CHUNKS = T // BANK
+Q_TILES = Q // P
+E_TILES = E // P
+KEY_LOADS = 2
+GAIN_ROW = M // P
+
+
+def tile_attend_difference_bymember_lean_kernel(
+    tc, query, keys_words, keys_scales, factors, vals, member, mgain, offs, offs2, offs3, out
+):
+    nc = tc.nc
+    with ExitStack() as ctx:
+        keep = ctx.enter_context(tc.tile_pool(name="keep", bufs=1))
+        acc_pool = ctx.enter_context(tc.psum_pool(name="acc", bufs=4))
+        turn_pool = ctx.enter_context(tc.psum_pool(name="turn", bufs=4))
+
+        key_planes = keep.tile([P, BANK], U8, name="key_planes", align_bytes=64)
+        nc.vector.memset(key_planes[:].bitcast(I32), 0)
+        ones = keep.tile([P, P], F32, name="ones")
+        nc.vector.memset(ones[:], 1.0)
+        ramp = keep.tile([P, P], F32, name="ramp", align_bytes=64)
+        nc.vector.tensor_tensor_scan(ramp[:], ones[:], ones[:], 0.0, ALU.mult, ALU.add)
+        ramp_turned = keep.tile([P, P], F32, name="ramp_turned", align_bytes=64)
+        nc.vector.transpose(ramp_turned[:], ramp[:])
+        ident = keep.tile([P, P], F32, name="ident")
+        for quad in range(4):
+            rows = slice(32 * quad, 32 * quad + 32)
+            nc.vector.tensor_scalar(
+                ident[rows, :], ramp[rows, :], ramp_turned[rows, 32 * quad : 32 * quad + 1], None, ALU.is_equal
+            )
+
+        list3 = keep.tile([P, Q // 16], U16, name="list3")
+        nc.sync.dma_start(list3[:], offs3)
+        q_raw = keep.tile([P, PACK, Q], F32, name="q_raw")
+        nc.sync.dma_start(out=q_raw[:], in_=query.rearrange("(p t) q -> p t q", t=PACK))
+
+        gain_parts = keep.tile([P, GAIN_ROW], F32, name="gain_parts")
+        nc.scalar.dma_start(out=gain_parts[:], in_=mgain[0:1, :].rearrange("o (p j) -> (o p) j", j=GAIN_ROW))
+
+        scale_rows = keys_scales[0].bitcast(I32).rearrange("r (k c) -> k r c", k=CHUNKS)
+        for quad in range(4):
+            nc.scalar.dma_start(
+                out=key_planes[32 * quad : 32 * quad + 16, :].bitcast(I32),
+                in_=scale_rows[:, 4 * quad : 4 * quad + 4, :],
+            )
+
+        words_hbm = keys_words[0].rearrange("p n t -> p (n t)").bitcast(I32)
+        key_width = T // KEY_LOADS
+        key_words = []
+        for h in range(KEY_LOADS):
+            words = keep.tile([P, key_width], U32, name=f"key_words{h}", tag=f"key_words{h}", align_bytes=64)
+            nc.sync.dma_start(out=words[:].bitcast(I32), in_=words_hbm[:, h * key_width : (h + 1) * key_width])
+            key_words.append(words)
+
+        list2 = keep.tile([P, I // 16], U16, name="list2")
+        nc.sync.dma_start(list2[:], offs2)
+        list1 = keep.tile([P, I // 16], U16, name="list1")
+        nc.sync.dma_start(list1[:], offs)
+
+        slot_factor = keep.tile([P, 1, PACK], F32, name="slot_factor")
+        val_pool = []
+        for j in range(E_TILES):
+            block = keep.tile([P, T], F32, name=f"val_pool{j}", tag=f"val_pool{j}", align_bytes=64)
+            nc.sync.dma_start(out=block[:], in_=vals[j * P : (j + 1) * P, :])
+            val_pool.append(block)
+            if j == 0:
+                nc.sync.dma_start(out=slot_factor[:, 0, :], in_=factors.rearrange("o (p t) -> (o p) t", t=PACK))
+        member_pool = []
+        for j in range(E_TILES):
+            block = keep.tile([P, M], F32, name=f"member_pool{j}", tag=f"member_pool{j}", align_bytes=64)
+            nc.sync.dma_start(out=block[:], in_=member[j * P : (j + 1) * P, :])
+            member_pool.append(block)
+
+        q_bf = [keep.tile([P, P, PACK], BF16, name=f"q_bf{g}", align_bytes=64) for g in range(Q_TILES)]
+        q_words = [keep.tile([P, P], U32, name=f"q_words{g}", align_bytes=64) for g in range(Q_TILES)]
+        q_plane = [keep.tile([P, P], U8, name=f"q_plane{g}", align_bytes=64) for g in range(Q_TILES)]
+        for g in range(Q_TILES):
+            nc.vector.tensor_copy(
+                out=q_bf[g][:].rearrange("p (c i) t -> p c t i", i=4),
+                in_=q_raw[:, :, g * P : (g + 1) * P].rearrange("p t (c i) -> p c t i", i=4),
+            )
+        for g in range(Q_TILES):
+            nc.vector.quantize_mx(
+                out=q_words[g][:].bitcast(FP8X4), scales=q_plane[g][:], in_=q_bf[g][:].rearrange("p q t -> p (q t)")
+            )
+
+        gain_pool = keep.tile([P, M], F32, name="gain_pool")
+        gain_view = gain_pool[:].rearrange("x (p j) -> x p j", j=GAIN_ROW)
+        for half in range(GAIN_ROW // PACK):
+            bank = turn_pool.tile([P, PACK, P], F32, name="turn")
+            for jj in range(PACK):
+                j = half * PACK + jj
+                nc.tensor.transpose(bank[:, jj, :], gain_parts[:, j : j + 1].to_broadcast([P, P]), ident[:])
+            nc.scalar.copy(
+                out=gain_view[:, :, half * PACK : (half + 1) * PACK], in_=bank[:].rearrange("x j p -> x p j")
+            )
+        gain = keep.tile([P, 1, Q], F32, name="gain")
+        nc.scalar.activation(gain[:, 0, :], gain_pool[:].indirect(list3[:]), COPY)
+
+        scores = [keep.tile([P, T], F32, name=f"scores{g}", tag=f"scores{g}") for g in range(Q_TILES)]
+        second = [keep.tile([P, I], F32, name=f"second{g}", tag=f"second{g}") for g in range(Q_TILES)]
+        diff = {}
+        picked = {}
+        picked_tag = ["second0", "scores0", "picked2", "picked3"]
+        w_bf = keep.tile([P, Q, PACK], BF16, name="w_bf", align_bytes=64)
+        w_words = keep.tile([P, Q], U32, name="w_words", align_bytes=64)
+        w_plane = keep.tile([P, Q], U8, name="w_plane", align_bytes=64)
+        turned = {}
+        v_bf = {}
+        v_words = {}
+        v_plane = {}
+        gained = {}
+        per_load = CHUNKS // KEY_LOADS
+
+        def score(g, on_scalar):
+            for c in range(CHUNKS):
+                h, cc = divmod(c, per_load)
+                bank = acc_pool.tile([P, BANK], F32, name="acc")
+                nc.tensor.matmul_mx(
+                    out=bank[:],
+                    lhsT=q_words[g][:].bitcast(FP8X4),
+                    lhsT_scale=q_plane[g][:],
+                    rhs=key_words[h][:, cc * BANK : (cc + 1) * BANK].bitcast(FP8X4),
+                    rhs_scale=key_planes[4 * c :, :],
+                    start=True,
+                    stop=True,
+                )
+                dst = scores[g][:, c * BANK : (c + 1) * BANK]
+                if c in on_scalar:
+                    nc.scalar.copy(out=dst, in_=bank[:])
+                else:
+                    nc.vector.tensor_copy(out=dst, in_=bank[:])
+
+        def look_up_second(g):
+            nc.scalar.activation(second[g][:], scores[g][:].indirect(list2[:]), COPY)
+
+        def subtract(g):
+            diff[g] = keep.tile([P, I], F32, name=f"diff{g}", tag=f"key_words{KEY_LOADS - 1 - g}", align_bytes=64)
+            nc.vector.tensor_tensor(diff[g][:], scores[g][:].indirect(list1[:]), second[g][:], ALU.subtract)
+
+        def weigh(g):
+            bank = turn_pool.tile([P, PACK, P], F32, name="turn")
+            for t in range(PACK):
+                nc.tensor.transpose(bank[:, t, :], diff[g][:, t::PACK], ident[:])
+            nc.vector.scalar_tensor_tensor(
+                out=w_bf[:, g * P : (g + 1) * P, :],
+                in0=bank[:].rearrange("p t q -> p q t"),
+                scalar=0.0,
+                in1=slot_factor[:].to_broadcast([P, P, PACK]),
+                op0=ALU.max,
+                op1=ALU.mult,
+            )
+
+        def pick(j):
+            picked[j] = keep.tile([P, I], BF16, name=f"picked{j}", tag=picked_tag[j])
+            nc.scalar.activation(picked[j][:], val_pool[j][:].indirect(list1[:]), COPY)
+
+        def turn_values(j):
+            pairs = picked[j][:].bitcast(F32)
+            turned[j] = turn_pool.tile([P, 2, P], F32, name="turn")
+            for u in range(2):
+                nc.tensor.transpose(turned[j][:, u, :], pairs[:, u::2], ident[:])
+
+        def lay_out_values(blocks, tag):
+            laid = keep.tile([P, len(blocks), P, PACK], BF16, name=f"v_bf{blocks[0]}", tag=tag, align_bytes=64)
+            for n, j in enumerate(blocks):
+                nc.scalar.copy(out=laid[:, n, :, :].bitcast(F32), in_=turned[j][:].rearrange("p u e -> p e u"))
+            v_bf[blocks] = laid
+
+        def quantise_values(blocks, tag):
+            width = len(blocks) * P
+            v_words[blocks] = keep.tile([P, width], U32, name=f"v_words{blocks[0]}", tag=tag, align_bytes=64)
+            v_plane[blocks] = keep.tile([P, width], U8, name=f"v_plane{blocks[0]}", align_bytes=64)
+            nc.vector.quantize_mx(
+                out=v_words[blocks][:].bitcast(FP8X4),
+                scales=v_plane[blocks][:],
+                in_=v_bf[blocks][:].rearrange("p n e t -> p (n e t)"),
+            )
+
+        def add_up(blocks, tag):
+            summed = acc_pool.tile([P, len(blocks), Q], F32, name="acc")
+            for n in range(len(blocks)):
+                nc.tensor.matmul_mx(
+                    out=summed[:, n, :],
+                    lhsT=v_words[blocks][:, n * P : (n + 1) * P].bitcast(FP8X4),
+                    lhsT_scale=v_plane[blocks][:, n * P : (n + 1) * P],
+                    rhs=w_words[:].bitcast(FP8X4),
+                    rhs_scale=w_plane[:],
+                    start=True,
+                    stop=True,
+                )
+            product = keep.tile([P, len(blocks), Q], F32, name=f"gained{blocks[0]}", tag=tag, align_bytes=64)
+            nc.vector.tensor_tensor(product[:], summed[:], gain[:].to_broadcast([P, len(blocks), Q]), ALU.mult)
+            for n, j in enumerate(blocks):
+                gained[j] = product[:, n, :]
+
+        def finish(j):
+            result = keep.tile([P, Q], F32, name=f"result{j}")
+            nc.vector.tensor_tensor(result[:], member_pool[j][:].indirect(list3[:]), gained[j], ALU.add)
+            nc.sync.dma_start(out=out[j * P : (j + 1) * P, :], in_=result[:])
+
+        score(0, (0, 2))
+        look_up_second(0)
+        score(1, (3,))
+        look_up_second(1)
+        subtract(0)
+        subtract(1)
+        pick(0)
+        pick(1)
+        weigh(0)
+        weigh(1)
+        turn_values(0)
+        nc.vector.quantize_mx(
+            out=w_words[:].bitcast(FP8X4), scales=w_plane[:], in_=w_bf[:].rearrange("p q t -> p (q t)")
+        )
+        lay_out_values((0,), "val_pool1")
+        turn_values(1)
+        pick(2)
+        quantise_values((0,), "v_words0")
+        lay_out_values((1,), "val_pool2")
+        turn_values(2)
+        pick(3)
+        add_up((0,), "gained0")
+        quantise_values((1,), "v_words1")
+        turn_values(3)
+        add_up((1,), "gained1")
+        lay_out_values((2, 3), "val_pool3")
+        finish(0)
+        quantise_values((2, 3), "member_pool0")
+        finish(1)
+        add_up((2, 3), "member_pool1")
+        finish(2)
+        finish(3)

@@ -21,7 +21,7 @@ BANK = 512
 CHUNKS = T // BANK
 Q_TILES = Q // P
 E_TILES = E // P
-KEY_LOADS = 2
+KEY_LOADS = ((0, 1), (2, 3))
 GAIN_ROW = M // P
 
 
@@ -31,11 +31,10 @@ def tile_attend_difference_bymember_lean_kernel(
     nc = tc.nc
     with ExitStack() as ctx:
         keep = ctx.enter_context(tc.tile_pool(name="keep", bufs=1))
-        acc_pool = ctx.enter_context(tc.psum_pool(name="acc", bufs=4))
-        turn_pool = ctx.enter_context(tc.psum_pool(name="turn", bufs=4))
+        banks = ctx.enter_context(tc.psum_pool(name="banks", bufs=8))
 
         key_planes = keep.tile([P, BANK], U8, name="key_planes", align_bytes=64)
-        nc.vector.memset(key_planes[:].bitcast(I32), 0)
+        nc.gpsimd.memset(key_planes[:].bitcast(I32), 0)
         ones = keep.tile([P, P], F32, name="ones")
         nc.vector.memset(ones[:], 1.0)
         ramp = keep.tile([P, P], F32, name="ramp", align_bytes=64)
@@ -65,17 +64,16 @@ def tile_attend_difference_bymember_lean_kernel(
             )
 
         words_hbm = keys_words[0].rearrange("p n t -> p (n t)").bitcast(I32)
-        key_width = T // KEY_LOADS
-        key_words = []
-        for h in range(KEY_LOADS):
-            words = keep.tile([P, key_width], U32, name=f"key_words{h}", tag=f"key_words{h}", align_bytes=64)
-            nc.sync.dma_start(out=words[:].bitcast(I32), in_=words_hbm[:, h * key_width : (h + 1) * key_width])
-            key_words.append(words)
+        key_words = {}
+        for h, chunks in enumerate(KEY_LOADS):
+            words = keep.tile([P, len(chunks) * BANK], U32, name=f"key_words{h}", tag=f"key_words{h}", align_bytes=64)
+            nc.sync.dma_start(out=words[:].bitcast(I32), in_=words_hbm[:, chunks[0] * BANK : (chunks[-1] + 1) * BANK])
+            for n, c in enumerate(chunks):
+                key_words[c] = words[:, n * BANK : (n + 1) * BANK]
 
         list2 = keep.tile([P, I // 16], U16, name="list2")
         nc.sync.dma_start(list2[:], offs2)
         list1 = keep.tile([P, I // 16], U16, name="list1")
-        nc.sync.dma_start(list1[:], offs)
 
         slot_factor = keep.tile([P, 1, PACK], F32, name="slot_factor")
         val_pool = []
@@ -84,6 +82,7 @@ def tile_attend_difference_bymember_lean_kernel(
             nc.sync.dma_start(out=block[:], in_=vals[j * P : (j + 1) * P, :])
             val_pool.append(block)
             if j == 0:
+                nc.sync.dma_start(list1[:], offs)
                 nc.sync.dma_start(out=slot_factor[:, 0, :], in_=factors.rearrange("o (p t) -> (o p) t", t=PACK))
         member_pool = []
         for j in range(E_TILES):
@@ -107,22 +106,20 @@ def tile_attend_difference_bymember_lean_kernel(
         gain_pool = keep.tile([P, M], F32, name="gain_pool")
         gain_view = gain_pool[:].rearrange("x (p j) -> x p j", j=GAIN_ROW)
         for half in range(GAIN_ROW // PACK):
-            bank = turn_pool.tile([P, PACK, P], F32, name="turn")
+            bank = banks.tile([P, PACK, P], F32, name="bank")
             for jj in range(PACK):
                 j = half * PACK + jj
                 nc.tensor.transpose(bank[:, jj, :], gain_parts[:, j : j + 1].to_broadcast([P, P]), ident[:])
             nc.scalar.copy(
                 out=gain_view[:, :, half * PACK : (half + 1) * PACK], in_=bank[:].rearrange("x j p -> x p j")
             )
-        gain = keep.tile([P, 1, Q], F32, name="gain")
-        nc.scalar.activation(gain[:, 0, :], gain_pool[:].indirect(list3[:]), COPY)
 
-        scores = [keep.tile([P, T], F32, name=f"scores{g}", tag=f"scores{g}") for g in range(Q_TILES)]
-        second = [keep.tile([P, I], F32, name=f"second{g}", tag=f"second{g}") for g in range(Q_TILES)]
+        scores = [keep.tile([P, T], F32, name=f"scores{g}", tag=f"scores{g}", align_bytes=64) for g in range(Q_TILES)]
+        second = {}
+        second_tag = ["key_words1", "second1"]
         diff = {}
         picked = {}
-        picked_tag = ["second0", "scores0", "picked2", "picked3"]
-        w_bf = keep.tile([P, Q, PACK], BF16, name="w_bf", align_bytes=64)
+        picked_tag = ["picked0", "picked1", "picked2", "picked3"]
         w_words = keep.tile([P, Q], U32, name="w_words", align_bytes=64)
         w_plane = keep.tile([P, Q], U8, name="w_plane", align_bytes=64)
         turned = {}
@@ -130,36 +127,38 @@ def tile_attend_difference_bymember_lean_kernel(
         v_words = {}
         v_plane = {}
         gained = {}
-        per_load = CHUNKS // KEY_LOADS
 
-        def score(g, on_scalar):
-            for c in range(CHUNKS):
-                h, cc = divmod(c, per_load)
-                bank = acc_pool.tile([P, BANK], F32, name="acc")
+        def score(g, chunks):
+            for c in chunks:
+                bank = banks.tile([P, BANK], F32, name="bank")
                 nc.tensor.matmul_mx(
                     out=bank[:],
                     lhsT=q_words[g][:].bitcast(FP8X4),
                     lhsT_scale=q_plane[g][:],
-                    rhs=key_words[h][:, cc * BANK : (cc + 1) * BANK].bitcast(FP8X4),
+                    rhs=key_words[c].bitcast(FP8X4),
                     rhs_scale=key_planes[4 * c :, :],
                     start=True,
                     stop=True,
                 )
                 dst = scores[g][:, c * BANK : (c + 1) * BANK]
-                if c in on_scalar:
+                if c % 2 == 0:
                     nc.scalar.copy(out=dst, in_=bank[:])
                 else:
                     nc.vector.tensor_copy(out=dst, in_=bank[:])
 
         def look_up_second(g):
-            nc.scalar.activation(second[g][:], scores[g][:].indirect(list2[:]), COPY)
+            second[g] = keep.tile([P, I], F32, name=f"second{g}", tag=second_tag[g], align_bytes=64)
+            if g == 0:
+                nc.scalar.activation(second[g][:], scores[g][:].indirect(list2[:]), COPY)
+            else:
+                nc.vector.tensor_copy(second[g][:], scores[g][:].indirect(list2[:]))
 
         def subtract(g):
-            diff[g] = keep.tile([P, I], F32, name=f"diff{g}", tag=f"key_words{KEY_LOADS - 1 - g}", align_bytes=64)
+            diff[g] = keep.tile([P, I], F32, name=f"diff{g}")
             nc.vector.tensor_tensor(diff[g][:], scores[g][:].indirect(list1[:]), second[g][:], ALU.subtract)
 
-        def weigh(g):
-            bank = turn_pool.tile([P, PACK, P], F32, name="turn")
+        def weigh(g, w_bf):
+            bank = banks.tile([P, PACK, P], F32, name="bank")
             for t in range(PACK):
                 nc.tensor.transpose(bank[:, t, :], diff[g][:, t::PACK], ident[:])
             nc.vector.scalar_tensor_tensor(
@@ -172,19 +171,19 @@ def tile_attend_difference_bymember_lean_kernel(
             )
 
         def pick(j):
-            picked[j] = keep.tile([P, I], BF16, name=f"picked{j}", tag=picked_tag[j])
+            picked[j] = keep.tile([P, I], BF16, name=f"picked{j}", tag=picked_tag[j], align_bytes=64)
             nc.scalar.activation(picked[j][:], val_pool[j][:].indirect(list1[:]), COPY)
 
         def turn_values(j):
             pairs = picked[j][:].bitcast(F32)
-            turned[j] = turn_pool.tile([P, 2, P], F32, name="turn")
+            turned[j] = banks.tile([P, 2, P], F32, name="bank")
             for u in range(2):
                 nc.tensor.transpose(turned[j][:, u, :], pairs[:, u::2], ident[:])
 
-        def lay_out_values(blocks, tag):
+        def lay_out_values(blocks, tag, copy):
             laid = keep.tile([P, len(blocks), P, PACK], BF16, name=f"v_bf{blocks[0]}", tag=tag, align_bytes=64)
             for n, j in enumerate(blocks):
-                nc.scalar.copy(out=laid[:, n, :, :].bitcast(F32), in_=turned[j][:].rearrange("p u e -> p e u"))
+                copy(laid[:, n, :, :].bitcast(F32), turned[j][:].rearrange("p u e -> p e u"))
             v_bf[blocks] = laid
 
         def quantise_values(blocks, tag):
@@ -198,7 +197,7 @@ def tile_attend_difference_bymember_lean_kernel(
             )
 
         def add_up(blocks, tag):
-            summed = acc_pool.tile([P, len(blocks), Q], F32, name="acc")
+            summed = banks.tile([P, len(blocks), Q], F32, name="bank")
             for n in range(len(blocks)):
                 nc.tensor.matmul_mx(
                     out=summed[:, n, :],
@@ -216,35 +215,41 @@ def tile_attend_difference_bymember_lean_kernel(
 
         def finish(j):
             result = keep.tile([P, Q], F32, name=f"result{j}")
-            nc.vector.tensor_tensor(result[:], member_pool[j][:].indirect(list3[:]), gained[j], ALU.add)
+            listed = member_pool[j][:].indirect(list3[:])
+            if j == 2:
+                columns = keep.tile([P, Q], F32, name="columns")
+                nc.scalar.activation(columns[:], listed, COPY)
+                listed = columns[:]
+            nc.vector.tensor_tensor(result[:], listed, gained[j], ALU.add)
             nc.sync.dma_start(out=out[j * P : (j + 1) * P, :], in_=result[:])
 
-        score(0, (0, 2))
+        for chunks in KEY_LOADS:
+            for g in range(Q_TILES):
+                score(g, chunks)
         look_up_second(0)
-        score(1, (3,))
         look_up_second(1)
         subtract(0)
         subtract(1)
         pick(0)
         pick(1)
-        weigh(0)
-        weigh(1)
+        w_bf = keep.tile([P, Q, PACK], BF16, name="w_bf", align_bytes=64)
         turn_values(0)
+        weigh(0, w_bf)
+        gain = keep.tile([P, 1, Q], F32, name="gain", tag="second1", align_bytes=64)
+        nc.vector.tensor_copy(gain[:, 0, :], gain_pool[:].indirect(list3[:]))
+        weigh(1, w_bf)
         nc.vector.quantize_mx(
             out=w_words[:].bitcast(FP8X4), scales=w_plane[:], in_=w_bf[:].rearrange("p q t -> p (q t)")
         )
-        lay_out_values((0,), "val_pool1")
         turn_values(1)
         pick(2)
-        quantise_values((0,), "v_words0")
-        lay_out_values((1,), "val_pool2")
         turn_values(2)
+        lay_out_values((0, 1), "val_pool2", nc.scalar.copy)
         pick(3)
-        add_up((0,), "gained0")
-        quantise_values((1,), "v_words1")
+        quantise_values((0, 1), "v_words0")
         turn_values(3)
-        add_up((1,), "gained1")
-        lay_out_values((2, 3), "val_pool3")
+        add_up((0, 1), "gained0")
+        lay_out_values((2, 3), "val_pool3", nc.scalar.copy)
         finish(0)
         quantise_values((2, 3), "member_pool0")
         finish(1)

@@ -216,8 +216,8 @@ def tile_attend_difference_bymember_lean_kernel(
         def finish(j):
             result = keep.tile([P, Q], F32, name=f"result{j}")
             listed = member_pool[j][:].indirect(list3[:])
-            if j == 2:
-                columns = keep.tile([P, Q], F32, name="columns")
+            if j in (1, 2):
+                columns = keep.tile([P, Q], F32, name=f"columns{j}", tag=f"columns{j}", align_bytes=64)
                 nc.scalar.activation(columns[:], listed, COPY)
                 listed = columns[:]
             nc.vector.tensor_tensor(result[:], listed, gained[j], ALU.add)
@@ -231,12 +231,12 @@ def tile_attend_difference_bymember_lean_kernel(
         subtract(0)
         subtract(1)
         pick(0)
+        gain = keep.tile([P, 1, Q], F32, name="gain", tag="val_pool0", align_bytes=64)
+        nc.scalar.activation(gain[:, 0, :], gain_pool[:].indirect(list3[:]), COPY)
         pick(1)
         w_bf = keep.tile([P, Q, PACK], BF16, name="w_bf", align_bytes=64)
         turn_values(0)
         weigh(0, w_bf)
-        gain = keep.tile([P, 1, Q], F32, name="gain", tag="second1", align_bytes=64)
-        nc.vector.tensor_copy(gain[:, 0, :], gain_pool[:].indirect(list3[:]))
         weigh(1, w_bf)
         nc.vector.quantize_mx(
             out=w_words[:].bitcast(FP8X4), scales=w_plane[:], in_=w_bf[:].rearrange("p q t -> p (q t)")
@@ -249,10 +249,13 @@ def tile_attend_difference_bymember_lean_kernel(
         quantise_values((0, 1), "v_words0")
         turn_values(3)
         add_up((0, 1), "gained0")
-        lay_out_values((2, 3), "val_pool3", nc.scalar.copy)
+        lay_out_values((2,), "val_pool3", nc.scalar.copy)
+        lay_out_values((3,), "v_bf3", nc.scalar.copy)
+        quantise_values((2,), "v_words2")
+        quantise_values((3,), "v_words3")
+        add_up((2,), "gained2")
         finish(0)
-        quantise_values((2, 3), "member_pool0")
         finish(1)
-        add_up((2, 3), "member_pool1")
+        add_up((3,), "columns1")
         finish(2)
         finish(3)

@@ -31,7 +31,7 @@ def tile_attend_difference_bymember_lean_kernel(
     nc = tc.nc
     with ExitStack() as ctx:
         keep = ctx.enter_context(tc.tile_pool(name="keep", bufs=1))
-        banks = ctx.enter_context(tc.psum_pool(name="banks", bufs=8))
+        banks = ctx.enter_context(tc.psum_pool(name="banks", bufs=1))
 
         key_planes = keep.tile([P, BANK], U8, name="key_planes", align_bytes=64)
         nc.gpsimd.memset(key_planes[:].bitcast(I32), 0)
@@ -106,20 +106,22 @@ def tile_attend_difference_bymember_lean_kernel(
         gain_pool = keep.tile([P, M], F32, name="gain_pool")
         gain_view = gain_pool[:].rearrange("x (p j) -> x p j", j=GAIN_ROW)
         for half in range(GAIN_ROW // PACK):
-            bank = banks.tile([P, PACK, P], F32, name="bank")
+            bank = banks.tile([P, PACK, P], F32, name=f"gain_turned{half}", tag=f"bank{6 + half}")
             for jj in range(PACK):
                 j = half * PACK + jj
                 nc.tensor.transpose(bank[:, jj, :], gain_parts[:, j : j + 1].to_broadcast([P, P]), ident[:])
             nc.scalar.copy(
                 out=gain_view[:, :, half * PACK : (half + 1) * PACK], in_=bank[:].rearrange("x j p -> x p j")
             )
+        gain = keep.tile([P, 1, Q], F32, name="gain")
+        nc.scalar.activation(gain[:, 0, :], gain_pool[:].indirect(list3[:]), COPY)
 
         scores = [keep.tile([P, T], F32, name=f"scores{g}", tag=f"scores{g}", align_bytes=64) for g in range(Q_TILES)]
         second = {}
-        second_tag = ["key_words1", "second1"]
         diff = {}
+        diff_turned = {}
+        w_bf = {}
         picked = {}
-        picked_tag = ["picked0", "picked1", "picked2", "picked3"]
         w_words = keep.tile([P, Q], U32, name="w_words", align_bytes=64)
         w_plane = keep.tile([P, Q], U8, name="w_plane", align_bytes=64)
         turned = {}
@@ -127,82 +129,80 @@ def tile_attend_difference_bymember_lean_kernel(
         v_words = {}
         v_plane = {}
         gained = {}
+        columns = {}
 
-        def score(g, chunks):
-            for c in chunks:
-                bank = banks.tile([P, BANK], F32, name="bank")
-                nc.tensor.matmul_mx(
-                    out=bank[:],
-                    lhsT=q_words[g][:].bitcast(FP8X4),
-                    lhsT_scale=q_plane[g][:],
-                    rhs=key_words[c].bitcast(FP8X4),
-                    rhs_scale=key_planes[4 * c :, :],
-                    start=True,
-                    stop=True,
-                )
-                dst = scores[g][:, c * BANK : (c + 1) * BANK]
-                if c % 2 == 0:
-                    nc.scalar.copy(out=dst, in_=bank[:])
-                else:
-                    nc.vector.tensor_copy(out=dst, in_=bank[:])
+        def score(g, c, bank_no, copy):
+            bank = banks.tile([P, BANK], F32, name=f"score{g}_{c}", tag=f"bank{bank_no}")
+            nc.tensor.matmul_mx(
+                out=bank[:],
+                lhsT=q_words[g][:].bitcast(FP8X4),
+                lhsT_scale=q_plane[g][:],
+                rhs=key_words[c].bitcast(FP8X4),
+                rhs_scale=key_planes[4 * c :, :],
+                start=True,
+                stop=True,
+            )
+            copy(scores[g][:, c * BANK : (c + 1) * BANK], bank[:])
 
         def look_up_second(g):
-            second[g] = keep.tile([P, I], F32, name=f"second{g}", tag=second_tag[g], align_bytes=64)
-            if g == 0:
-                nc.scalar.activation(second[g][:], scores[g][:].indirect(list2[:]), COPY)
-            else:
-                nc.vector.tensor_copy(second[g][:], scores[g][:].indirect(list2[:]))
+            second[g] = keep.tile([P, I], F32, name=f"second{g}", align_bytes=64)
+            nc.vector.tensor_copy(second[g][:], scores[g][:].indirect(list2[:]))
 
         def subtract(g):
             diff[g] = keep.tile([P, I], F32, name=f"diff{g}")
             nc.vector.tensor_tensor(diff[g][:], scores[g][:].indirect(list1[:]), second[g][:], ALU.subtract)
 
-        def weigh(g, w_bf):
-            bank = banks.tile([P, PACK, P], F32, name="bank")
+        def turn_diff(g, bank_no):
+            diff_turned[g] = banks.tile([P, PACK, P], F32, name=f"diff_turned{g}", tag=f"bank{bank_no}")
             for t in range(PACK):
-                nc.tensor.transpose(bank[:, t, :], diff[g][:, t::PACK], ident[:])
+                nc.tensor.transpose(diff_turned[g][:, t, :], diff[g][:, t::PACK], ident[:])
+
+        def weigh(g, tag):
+            w_bf[g] = keep.tile([P, P, PACK], BF16, name=f"w_bf{g}", tag=tag, align_bytes=64)
             nc.vector.scalar_tensor_tensor(
-                out=w_bf[:, g * P : (g + 1) * P, :],
-                in0=bank[:].rearrange("p t q -> p q t"),
+                out=w_bf[g][:],
+                in0=diff_turned[g][:].rearrange("p t q -> p q t"),
                 scalar=0.0,
                 in1=slot_factor[:].to_broadcast([P, P, PACK]),
                 op0=ALU.max,
                 op1=ALU.mult,
             )
 
-        def pick(j):
-            picked[j] = keep.tile([P, I], BF16, name=f"picked{j}", tag=picked_tag[j], align_bytes=64)
+        def quantise_weights(g):
+            nc.vector.quantize_mx(
+                out=w_words[:, g * P : (g + 1) * P].bitcast(FP8X4),
+                scales=w_plane[:, g * P : (g + 1) * P],
+                in_=w_bf[g][:].rearrange("p q t -> p (q t)"),
+            )
+
+        def pick(j, tag):
+            picked[j] = keep.tile([P, I], BF16, name=f"picked{j}", tag=tag, align_bytes=64)
             nc.scalar.activation(picked[j][:], val_pool[j][:].indirect(list1[:]), COPY)
 
-        def turn_values(j):
+        def turn_values(j, bank_no):
             pairs = picked[j][:].bitcast(F32)
-            turned[j] = banks.tile([P, 2, P], F32, name="bank")
+            turned[j] = banks.tile([P, 2, P], F32, name=f"turned{j}", tag=f"bank{bank_no}")
             for u in range(2):
                 nc.tensor.transpose(turned[j][:, u, :], pairs[:, u::2], ident[:])
 
-        def lay_out_values(blocks, tag, copy):
-            laid = keep.tile([P, len(blocks), P, PACK], BF16, name=f"v_bf{blocks[0]}", tag=tag, align_bytes=64)
-            for n, j in enumerate(blocks):
-                copy(laid[:, n, :, :].bitcast(F32), turned[j][:].rearrange("p u e -> p e u"))
-            v_bf[blocks] = laid
+        def lay_out_values(j, tag):
+            v_bf[j] = keep.tile([P, P, PACK], BF16, name=f"v_bf{j}", tag=tag, align_bytes=64)
+            nc.scalar.copy(v_bf[j][:].bitcast(F32), turned[j][:].rearrange("p u e -> p e u"))
 
-        def quantise_values(blocks, tag):
-            width = len(blocks) * P
-            v_words[blocks] = keep.tile([P, width], U32, name=f"v_words{blocks[0]}", tag=tag, align_bytes=64)
-            v_plane[blocks] = keep.tile([P, width], U8, name=f"v_plane{blocks[0]}", align_bytes=64)
+        def quantise_values(j):
+            v_words[j] = keep.tile([P, P], U32, name=f"v_words{j}", align_bytes=64)
+            v_plane[j] = keep.tile([P, P], U8, name=f"v_plane{j}", align_bytes=64)
             nc.vector.quantize_mx(
-                out=v_words[blocks][:].bitcast(FP8X4),
-                scales=v_plane[blocks][:],
-                in_=v_bf[blocks][:].rearrange("p n e t -> p (n e t)"),
+                out=v_words[j][:].bitcast(FP8X4), scales=v_plane[j][:], in_=v_bf[j][:].rearrange("p e t -> p (e t)")
             )
 
-        def add_up(blocks, tag):
-            summed = banks.tile([P, len(blocks), Q], F32, name="bank")
-            for n in range(len(blocks)):
+        def add_up(blocks, bank_no, tag):
+            summed = banks.tile([P, len(blocks), Q], F32, name=f"summed{blocks[0]}", tag=f"bank{bank_no}")
+            for n, j in enumerate(blocks):
                 nc.tensor.matmul_mx(
                     out=summed[:, n, :],
-                    lhsT=v_words[blocks][:, n * P : (n + 1) * P].bitcast(FP8X4),
-                    lhsT_scale=v_plane[blocks][:, n * P : (n + 1) * P],
+                    lhsT=v_words[j][:].bitcast(FP8X4),
+                    lhsT_scale=v_plane[j][:],
                     rhs=w_words[:].bitcast(FP8X4),
                     rhs_scale=w_plane[:],
                     start=True,
@@ -213,49 +213,58 @@ def tile_attend_difference_bymember_lean_kernel(
             for n, j in enumerate(blocks):
                 gained[j] = product[:, n, :]
 
-        def finish(j):
+        def gather_members(j):
+            columns[j] = keep.tile([P, Q], F32, name=f"columns{j}", tag=f"columns{j}", align_bytes=64)
+            nc.scalar.activation(columns[j][:], member_pool[j][:].indirect(list3[:]), COPY)
+
+        def finish(j, listed):
             result = keep.tile([P, Q], F32, name=f"result{j}")
-            listed = member_pool[j][:].indirect(list3[:])
-            if j in (1, 2):
-                columns = keep.tile([P, Q], F32, name=f"columns{j}", tag=f"columns{j}", align_bytes=64)
-                nc.scalar.activation(columns[:], listed, COPY)
-                listed = columns[:]
             nc.vector.tensor_tensor(result[:], listed, gained[j], ALU.add)
             nc.sync.dma_start(out=out[j * P : (j + 1) * P, :], in_=result[:])
 
-        for chunks in KEY_LOADS:
-            for g in range(Q_TILES):
-                score(g, chunks)
+        on_scalar = nc.scalar.copy
+        on_vector = nc.vector.tensor_copy
+        score(0, 0, 0, on_scalar)
+        score(0, 1, 1, on_vector)
+        score(0, 2, 2, on_scalar)
+        score(0, 3, 3, on_vector)
         look_up_second(0)
-        look_up_second(1)
+        score(1, 2, 4, on_scalar)
+        score(1, 3, 5, on_scalar)
+        score(1, 0, 2, on_scalar)
+        score(1, 1, 3, on_scalar)
         subtract(0)
+        look_up_second(1)
         subtract(1)
-        pick(0)
-        gain = keep.tile([P, 1, Q], F32, name="gain", tag="val_pool0", align_bytes=64)
-        nc.scalar.activation(gain[:, 0, :], gain_pool[:].indirect(list3[:]), COPY)
-        pick(1)
-        w_bf = keep.tile([P, Q, PACK], BF16, name="w_bf", align_bytes=64)
-        turn_values(0)
-        weigh(0, w_bf)
-        weigh(1, w_bf)
-        nc.vector.quantize_mx(
-            out=w_words[:].bitcast(FP8X4), scales=w_plane[:], in_=w_bf[:].rearrange("p q t -> p (q t)")
-        )
-        turn_values(1)
-        pick(2)
-        turn_values(2)
-        lay_out_values((0, 1), "val_pool2", nc.scalar.copy)
-        pick(3)
-        quantise_values((0, 1), "v_words0")
-        turn_values(3)
-        add_up((0, 1), "gained0")
-        lay_out_values((2,), "val_pool3", nc.scalar.copy)
-        lay_out_values((3,), "v_bf3", nc.scalar.copy)
-        quantise_values((2,), "v_words2")
-        quantise_values((3,), "v_words3")
-        add_up((2,), "gained2")
-        finish(0)
-        finish(1)
-        add_up((3,), "columns1")
-        finish(2)
-        finish(3)
+        pick(0, "key_words0")
+        turn_diff(0, 0)
+        turn_values(0, 6)
+        pick(1, "picked1")
+        turn_values(1, 7)
+        lay_out_values(0, "val_pool1")
+        turn_diff(1, 6)
+        weigh(0, "scores1")
+        quantise_values(0)
+        quantise_weights(0)
+        weigh(1, "w_bf1")
+        pick(2, "picked2")
+        turn_values(2, 0)
+        lay_out_values(1, "val_pool2")
+        lay_out_values(2, "v_bf2")
+        quantise_values(1)
+        quantise_weights(1)
+        quantise_values(2)
+        pick(3, "picked3")
+        add_up((0, 1), 7, "gained0")
+        add_up((2,), 5, "gained2")
+        gather_members(0)
+        turn_values(3, 6)
+        lay_out_values(3, "member_pool0")
+        finish(0, columns[0][:])
+        quantise_values(3)
+        gather_members(1)
+        finish(1, columns[1][:])
+        add_up((3,), 3, "columns1")
+        gather_members(2)
+        finish(2, columns[2][:])
+        finish(3, member_pool[3][:].indirect(list3[:]))

from contextlib import ExitStack

import concourse.mybir as mybir

D, T, I, Q, E, M = 512, 2048, 512, 256, 512, 1024
FLOPS = 2 * D * Q * T + 2 * I * E * Q

F32 = mybir.dt.float32
BF16 = mybir.dt.bfloat16
I32 = mybir.dt.int32
U32 = mybir.dt.uint32
U16 = mybir.dt.uint16
U8 = mybir.dt.uint8
FP8X4 = mybir.dt.float8_e4m3fn_x4
ALU = mybir.AluOpType
COPY = mybir.ActivationFunctionType.Copy

P = 128
PACK = 4
BANK = 512
CHUNKS = T // BANK
Q_TILES = Q // P
E_TILES = E // P
KEY_LOADS = ((0, 1), (2, 3))
GAIN_ROW = M // P


def tile_attend_difference_bymember_lean_kernel(
    tc, query, keys_words, keys_scales, factors, vals, member, mgain, offs, offs2, offs3, out
):
    nc = tc.nc
    with ExitStack() as ctx:
        keep = ctx.enter_context(tc.tile_pool(name="keep", bufs=1))
        banks = ctx.enter_context(tc.psum_pool(name="banks", bufs=1))

        key_planes = keep.tile([P, BANK], U8, name="key_planes", align_bytes=64)
        nc.gpsimd.memset(key_planes[:].bitcast(I32), 0)
        ones = keep.tile([P, P], F32, name="ones")
        nc.vector.memset(ones[:], 1.0)
        ramp = keep.tile([P, P], F32, name="ramp", align_bytes=64)
        nc.vector.tensor_tensor_scan(ramp[:], ones[:], ones[:], 0.0, ALU.mult, ALU.add)
        ramp_turned = keep.tile([P, P], F32, name="ramp_turned", align_bytes=64)
        nc.vector.transpose(ramp_turned[:], ramp[:])
        ident = keep.tile([P, P], F32, name="ident")
        for quad in range(4):
            rows = slice(32 * quad, 32 * quad + 32)
            nc.vector.tensor_scalar(
                ident[rows, :], ramp[rows, :], ramp_turned[rows, 32 * quad : 32 * quad + 1], None, ALU.is_equal
            )

        list3 = keep.tile([P, Q // 16], U16, name="list3")
        nc.sync.dma_start(list3[:], offs3)
        q_raw = keep.tile([P, PACK, Q], F32, name="q_raw")
        nc.sync.dma_start(out=q_raw[:], in_=query.rearrange("(p t) q -> p t q", t=PACK))

        gain_parts = keep.tile([P, GAIN_ROW], F32, name="gain_parts")
        nc.scalar.dma_start(out=gain_parts[:], in_=mgain[0:1, :].rearrange("o (p j) -> (o p) j", j=GAIN_ROW))

        scale_rows = keys_scales[0].bitcast(I32).rearrange("r (k c) -> k r c", k=CHUNKS)
        for quad in range(4):
            nc.scalar.dma_start(
                out=key_planes[32 * quad : 32 * quad + 16, :].bitcast(I32),
                in_=scale_rows[:, 4 * quad : 4 * quad + 4, :],
            )

        words_hbm = keys_words[0].rearrange("p n t -> p (n t)").bitcast(I32)
        key_words = {}
        for h, chunks in enumerate(KEY_LOADS):
            words = keep.tile([P, len(chunks) * BANK], U32, name=f"key_words{h}", tag=f"key_words{h}", align_bytes=64)
            nc.sync.dma_start(out=words[:].bitcast(I32), in_=words_hbm[:, chunks[0] * BANK : (chunks[-1] + 1) * BANK])
            for n, c in enumerate(chunks):
                key_words[c] = words[:, n * BANK : (n + 1) * BANK]

        list2 = keep.tile([P, I // 16], U16, name="list2")
        nc.sync.dma_start(list2[:], offs2)
        list1 = keep.tile([P, I // 16], U16, name="list1")

        slot_factor = keep.tile([P, 1, PACK], F32, name="slot_factor")
        val_pool = []
        for j in range(E_TILES):
            block = keep.tile([P, T], F32, name=f"val_pool{j}", tag=f"val_pool{j}", align_bytes=64)
            nc.sync.dma_start(out=block[:], in_=vals[j * P : (j + 1) * P, :])
            val_pool.append(block)
            if j == 0:
                nc.sync.dma_start(list1[:], offs)
                nc.sync.dma_start(out=slot_factor[:, 0, :], in_=factors.rearrange("o (p t) -> (o p) t", t=PACK))
        member_pool = []
        for j in range(E_TILES):
            block = keep.tile([P, M], F32, name=f"member_pool{j}", tag=f"member_pool{j}", align_bytes=64)
            nc.sync.dma_start(out=block[:], in_=member[j * P : (j + 1) * P, :])
            member_pool.append(block)

        q_bf = [keep.tile([P, P, PACK], BF16, name=f"q_bf{g}", align_bytes=64) for g in range(Q_TILES)]
        q_words = [keep.tile([P, P], U32, name=f"q_words{g}", align_bytes=64) for g in range(Q_TILES)]
        q_plane = [keep.tile([P, P], U8, name=f"q_plane{g}", align_bytes=64) for g in range(Q_TILES)]
        for g in range(Q_TILES):
            nc.vector.tensor_copy(
                out=q_bf[g][:].rearrange("p (c i) t -> p c t i", i=4),
                in_=q_raw[:, :, g * P : (g + 1) * P].rearrange("p t (c i) -> p c t i", i=4),
            )
        for g in range(Q_TILES):
            nc.vector.quantize_mx(
                out=q_words[g][:].bitcast(FP8X4), scales=q_plane[g][:], in_=q_bf[g][:].rearrange("p q t -> p (q t)")
            )

        gain_pool = keep.tile([P, M], F32, name="gain_pool")
        gain_view = gain_pool[:].rearrange("x (p j) -> x p j", j=GAIN_ROW)
        for half in range(GAIN_ROW // PACK):
            bank = banks.tile([P, PACK, P], F32, name=f"gain_turned{half}", tag=f"bank{6 + half}")
            for jj in range(PACK):
                j = half * PACK + jj
                nc.tensor.transpose(bank[:, jj, :], gain_parts[:, j : j + 1].to_broadcast([P, P]), ident[:])
            nc.scalar.copy(
                out=gain_view[:, :, half * PACK : (half + 1) * PACK], in_=bank[:].rearrange("x j p -> x p j")
            )
        gain = keep.tile([P, 1, Q], F32, name="gain")
        nc.scalar.activation(gain[:, 0, :], gain_pool[:].indirect(list3[:]), COPY)

        scores = [keep.tile([P, T], F32, name=f"scores{g}", tag=f"scores{g}", align_bytes=64) for g in range(Q_TILES)]
        second = {}
        diff = {}
        diff_turned = {}
        w_bf = {}
        picked = {}
        w_words = keep.tile([P, Q], U32, name="w_words", align_bytes=64)
        w_plane = keep.tile([P, Q], U8, name="w_plane", align_bytes=64)
        turned = {}
        v_bf = {}
        v_words = {}
        v_plane = {}
        gained = {}
        columns = {}

        def score(g, c, bank_no, copy):
            bank = banks.tile([P, BANK], F32, name=f"score{g}_{c}", tag=f"bank{bank_no}")
            nc.tensor.matmul_mx(
                out=bank[:],
                lhsT=q_words[g][:].bitcast(FP8X4),
                lhsT_scale=q_plane[g][:],
                rhs=key_words[c].bitcast(FP8X4),
                rhs_scale=key_planes[4 * c :, :],
                start=True,
                stop=True,
            )
            copy(scores[g][:, c * BANK : (c + 1) * BANK], bank[:])

        def look_up_second(g):
            second[g] = keep.tile([P, I], F32, name=f"second{g}", align_bytes=64)
            nc.vector.tensor_copy(second[g][:], scores[g][:].indirect(list2[:]))

        def subtract(g):
            diff[g] = keep.tile([P, I], F32, name=f"diff{g}")
            nc.vector.tensor_tensor(diff[g][:], scores[g][:].indirect(list1[:]), second[g][:], ALU.subtract)

        def turn_diff(g, bank_no):
            diff_turned[g] = banks.tile([P, PACK, P], F32, name=f"diff_turned{g}", tag=f"bank{bank_no}")
            for t in range(PACK):
                nc.tensor.transpose(diff_turned[g][:, t, :], diff[g][:, t::PACK], ident[:])

        def weigh(g, tag):
            w_bf[g] = keep.tile([P, P, PACK], BF16, name=f"w_bf{g}", tag=tag, align_bytes=64)
            nc.vector.scalar_tensor_tensor(
                out=w_bf[g][:],
                in0=diff_turned[g][:].rearrange("p t q -> p q t"),
                scalar=0.0,
                in1=slot_factor[:].to_broadcast([P, P, PACK]),
                op0=ALU.max,
                op1=ALU.mult,
            )

        def quantise_weights(g):
            nc.vector.quantize_mx(
                out=w_words[:, g * P : (g + 1) * P].bitcast(FP8X4),
                scales=w_plane[:, g * P : (g + 1) * P],
                in_=w_bf[g][:].rearrange("p q t -> p (q t)"),
            )

        def pick(j, tag):
            picked[j] = keep.tile([P, I], BF16, name=f"picked{j}", tag=tag, align_bytes=64)
            nc.scalar.activation(picked[j][:], val_pool[j][:].indirect(list1[:]), COPY)

        def turn_values(j, bank_no):
            pairs = picked[j][:].bitcast(F32)
            turned[j] = banks.tile([P, 2, P], F32, name=f"turned{j}", tag=f"bank{bank_no}")
            for u in range(2):
                nc.tensor.transpose(turned[j][:, u, :], pairs[:, u::2], ident[:])

        def lay_out_values(j, tag):
            v_bf[j] = keep.tile([P, P, PACK], BF16, name=f"v_bf{j}", tag=tag, align_bytes=64)
            nc.scalar.copy(v_bf[j][:].bitcast(F32), turned[j][:].rearrange("p u e -> p e u"))

        def quantise_values(j):
            v_words[j] = keep.tile([P, P], U32, name=f"v_words{j}", align_bytes=64)
            v_plane[j] = keep.tile([P, P], U8, name=f"v_plane{j}", align_bytes=64)
            nc.vector.quantize_mx(
                out=v_words[j][:].bitcast(FP8X4), scales=v_plane[j][:], in_=v_bf[j][:].rearrange("p e t -> p (e t)")
            )

        def add_up(blocks, bank_no, tag):
            summed = banks.tile([P, len(blocks), Q], F32, name=f"summed{blocks[0]}", tag=f"bank{bank_no}")
            for n, j in enumerate(blocks):
                nc.tensor.matmul_mx(
                    out=summed[:, n, :],
                    lhsT=v_words[j][:].bitcast(FP8X4),
                    lhsT_scale=v_plane[j][:],
                    rhs=w_words[:].bitcast(FP8X4),
                    rhs_scale=w_plane[:],
                    start=True,
                    stop=True,
                )
            product = keep.tile([P, len(blocks), Q], F32, name=f"gained{blocks[0]}", tag=tag, align_bytes=64)
            nc.vector.tensor_tensor(product[:], summed[:], gain[:].to_broadcast([P, len(blocks), Q]), ALU.mult)
            for n, j in enumerate(blocks):
                gained[j] = product[:, n, :]

        def gather_members(j):
            columns[j] = keep.tile([P, Q], F32, name=f"columns{j}", tag=f"columns{j}", align_bytes=64)
            nc.scalar.activation(columns[j][:], member_pool[j][:].indirect(list3[:]), COPY)

        def finish(j, listed):
            result = keep.tile([P, Q], F32, name=f"result{j}")
            nc.vector.tensor_tensor(result[:], listed, gained[j], ALU.add)
            nc.sync.dma_start(out=out[j * P : (j + 1) * P, :], in_=result[:])

        on_scalar = nc.scalar.copy
        on_vector = nc.vector.tensor_copy
        score(0, 0, 0, on_scalar)
        score(0, 1, 1, on_vector)
        score(0, 2, 2, on_scalar)
        score(0, 3, 3, on_vector)
        look_up_second(0)
        score(1, 2, 4, on_scalar)
        score(1, 3, 5, on_scalar)
        score(1, 0, 2, on_scalar)
        score(1, 1, 3, on_scalar)
        subtract(0)
        look_up_second(1)
        subtract(1)
        pick(0, "key_words0")
        turn_diff(0, 0)
        turn_values(0, 6)
        pick(1, "picked1")
        turn_values(1, 7)
        lay_out_values(0, "val_pool1")
        turn_diff(1, 6)
        weigh(0, "scores1")
        quantise_values(0)
        quantise_weights(0)
        weigh(1, "w_bf1")
        pick(2, "picked2")
        turn_values(2, 0)
        lay_out_values(1, "val_pool2")
        lay_out_values(2, "v_bf2")
        quantise_values(1)
        quantise_weights(1)
        quantise_values(2)
        pick(3, "picked3")
        add_up((0, 1), 7, "gained0")
        add_up((2,), 5, "gained2")
        gather_members(0)
        turn_values(3, 6)
        lay_out_values(3, "member_pool0")
        finish(0, columns[0][:])
        quantise_values(3)
        gather_members(1)
        finish(1, columns[1][:])
        add_up((3,), 3, "columns1")
        gather_members(2)
        finish(2, columns[2][:])
        finish(3, member_pool[3][:].indirect(list3[:]))
